import numpy as np
import ml_dtypes


def mxq(x, axis, fmt="e4m3"):
    dtype, down = {"e4m3": (ml_dtypes.float8_e4m3fn, 7), "e5m2": (ml_dtypes.float8_e5m2, 14)}[fmt]
    v = np.moveaxis(np.asarray(x, np.float32).astype(ml_dtypes.bfloat16).astype(np.float64), axis, -1)
    blocks = v.reshape(v.shape[:-1] + (-1, 32))
    amax = np.abs(blocks).max(-1, keepdims=True)
    byte = np.maximum(np.where(amax > 0, np.frexp(amax)[1] - 1 + 127, 0) - down, 1)
    scale = np.exp2(byte - 127.0)
    codes = (blocks / scale).astype(np.float32).astype(dtype).astype(np.float64)
    return np.moveaxis((codes * scale).reshape(v.shape), -1, axis)


WIDE = False


def mx_kscale(k):
    if not WIDE:
        return np.ones(k)
    levels = np.array([10, -10, 5, -5, 0])
    if k % 512:
        return np.exp2(np.random.permutation(np.resize(levels, k // 32))).repeat(32)
    a = np.empty((k // 512, 16))
    for p in range(k // 512):
        a[p, :8] = np.random.permutation(np.resize(levels, 8))
        for g in range(8):
            far = levels[np.abs(levels - a[p, g]) >= 10]
            a[p, g + 8] = far[np.random.randint(len(far))]
    return np.exp2(a.ravel()).repeat(32)


def f64(x):
    return np.asarray(x).astype(np.float64)


def striped(idx):
    return np.tile(idx.reshape(-1, 16).T, (8, 1)).astype(np.uint16)


def unstriped(offs):
    return offs[:16].T.reshape(-1).astype(np.int64)


def striped8(idx):
    return np.concatenate([x.reshape(-1, 16).T for x in idx]).astype(np.uint16)


def runs(offs, k):
    lists = np.stack([offs[16 * r : 16 * r + 16].T.reshape(-1) for r in range(8)]).astype(np.int64)
    return lists[np.arange(k) % 512 // 64]


def pack_weight(w):
    k, n = w.shape
    w = f64(np.asarray(w, np.float32).astype(ml_dtypes.bfloat16)).reshape(k // 32, 32, n)
    amax = np.abs(w).max(1)
    byte = np.clip(np.where(amax > 0, np.frexp(amax)[1] - 1 + 127 - 7, 1), 1, 254)
    scaled = (w * np.exp2(127.0 - byte)[:, None, :]).reshape(k, n).astype(np.float32)
    words = np.ascontiguousarray(scaled.reshape(k // 512, 128, 4, n).transpose(0, 1, 3, 2)).astype(ml_dtypes.float8_e4m3fn).view(np.uint8)
    return words, np.ascontiguousarray(byte.astype(np.uint8).reshape(k // 512, 16, n))


def unpack_weight(words, scales):
    g, p, n, _ = words.shape
    vals = np.ascontiguousarray(words).view(ml_dtypes.float8_e4m3fn).astype(np.float64) * np.repeat(np.exp2(scales.astype(np.float64) - 127.0), 8, axis=1)[..., None]
    return vals.transpose(0, 1, 3, 2).reshape(g * 512, n)


def sigmoid(v):
    return 1.0 / (1.0 + np.exp(-np.maximum(v, -700.0)))


K, T, S, N, H, J = 512, 2048, 512, 512, 512, 512


def setup_inputs():
    n = np.random.standard_normal
    s = mx_kscale(K)[:, None]
    u = mx_kscale(H)
    packed_xT = pack_weight(n((K, T)) * s)
    return {
        "x_words": packed_xT[0],
        "x_scales": packed_xT[1],
        "w1": (n((K, H)) / np.sqrt(K) / s).astype(np.float32),
        "tau": np.random.uniform(0.3, 0.9, (H, 1)).astype(np.float32),
        "tau2": np.random.uniform(0.3, 0.9, (H, 1)).astype(np.float32),
        "gn": (np.random.uniform(0.5, 1.5, (H, 1)) * u[:, None]).astype(np.float32),
        "w2": (n((H, N)) / np.sqrt(2 * H) / u[:, None]).astype(np.float32),
        "w3": (n((K, N)) / np.sqrt(2 * K) / s).astype(np.float32),
        "tab": n((N, J)).astype(np.float32),
        "sl": np.random.uniform(1.0, 2.0, (N, 1)).astype(np.float32),
        "th": (0.5 * n((N, 1))).astype(np.float32),
        "offs": striped8(np.random.randint(0, T, (8, S))),
        "n1": striped8(np.stack([np.random.permutation(S) for _ in range(8)])),
        "n2": striped8(np.stack([np.random.permutation(S) for _ in range(8)])),
        "two": striped(np.random.permutation(T)[:S]),
        "n3": striped(np.random.randint(0, J, S)),
        "n4": striped(np.random.permutation(S)),
    }


def reference(x_words, x_scales, w1, tau, tau2, gn, w2, w3, tab, sl, th, offs, n1, n2, two, n3, n4):
    xq = unpack_weight(x_words, x_scales)[np.arange(K)[:, None], runs(offs, K)]
    y = mxq(f64(w1), 0, "e4m3").T @ xq
    top = y.max(axis=1, keepdims=True)
    ea = np.exp(f64(tau) * (y[np.arange(H)[:, None], runs(n1, H)] - top))
    ea2 = np.exp(f64(tau2) * (y[np.arange(H)[:, None], runs(n2, H)] - top))
    z = f64(gn) * (0.5 * y + np.log((ea + 0.25) / (ea2 + 0.25)))
    x_two = unpack_weight(x_words, x_scales)[:, unstriped(two)]
    h = mxq(f64(w2), 0, "e4m3").T @ mxq(z, 0, "e4m3") + mxq(f64(w3), 0, "e4m3").T @ x_two
    sg = sigmoid(f64(sl) * (f64(tab)[:, unstriped(n3)] - f64(th)))
    return h * sg - (0.5 * h[:, unstriped(n4)])

@@ -1,0 +1,210 @@
+from contextlib import ExitStack
+
+import concourse.mybir as mybir
+
+K, T, S, N, H, J = 512, 2048, 512, 512, 512, 512
+FLOPS = 3 * 2 * 512 * 512 * 512
+
+F32 = mybir.dt.float32
+BF16 = mybir.dt.bfloat16
+I32 = mybir.dt.int32
+U32 = mybir.dt.uint32
+U16 = mybir.dt.uint16
+U8 = mybir.dt.uint8
+FP8X4 = mybir.dt.float8_e4m3fn_x4
+ALU = mybir.AluOpType
+ACT = mybir.ActivationFunctionType
+
+P = 128
+PACK = 4
+WIDE = 2 * S
+H_WINDOW = S + 16
+
+
+def tile_picked_hmixeosekd_none_p_kernel(
+    tc, x_words, x_scales, w1, tau, tau2, gn, w2, w3, tab, sl, th, offs, n1, n2, two, n3, n4, out
+):
+    nc = tc.nc
+    with ExitStack() as ctx:
+        keep = ctx.enter_context(tc.tile_pool(name="keep", bufs=1))
+        psum = ctx.enter_context(tc.psum_pool(name="psum", bufs=1))
+
+        def load_list(name, src):
+            dst = keep.tile([P, S // 16], U16, name=name)
+            nc.sync.dma_start(dst[:], src)
+            return dst
+
+        def load_column(queue, dst, src):
+            queue.dma_start(dst, src.rearrange("(p t) o -> p (t o)", t=PACK))
+
+        def load_weight(name, src):
+            raw = keep.tile([P, PACK, 512], F32, name=name, tag="weight_raw")
+            nc.sync.dma_start(raw[:], src.rearrange("(p j) c -> p j c", j=PACK))
+            return raw
+
+        def round_weight(name, raw):
+            grouped = keep.tile([P, PACK, P, PACK], BF16, name=name, align_bytes=64)
+            nc.vector.tensor_copy(
+                out=grouped[:].rearrange("p t m j -> p m j t"),
+                in_=raw[:].rearrange("p j (m t) -> p m j t", t=PACK),
+            )
+            return grouped
+
+        def quantize(name, grouped_ap):
+            codes = keep.tile([P, 512], U32, name=name + "_codes", align_bytes=64)
+            scales = keep.tile([P, 512], U8, name=name + "_scales", align_bytes=64)
+            nc.vector.quantize_mx(out=codes[:].bitcast(FP8X4), scales=scales[:], in_=grouped_ap)
+            return codes, scales
+
+        def mx(bank, weight, t, moving, start, stop):
+            cols = slice(t * P, (t + 1) * P)
+            nc.tensor.matmul_mx(
+                out=bank,
+                lhsT=weight[0][:, cols].bitcast(FP8X4),
+                lhsT_scale=weight[1][:, cols],
+                rhs=moving[0].bitcast(FP8X4),
+                rhs_scale=moving[1],
+                start=start,
+                stop=stop,
+            )
+
+        bytes_in = keep.tile([P, T], U8, name="bytes_in", align_bytes=64)
+        quarter = keep.tile([P, 1], F32, name="quarter")
+        nc.vector.memset(quarter[:], 0.25)
+
+        offs_t = load_list("offs_t", offs)
+        rows = x_scales[0].bitcast(I32).rearrange("(q r) c -> r q c", r=4)
+        for r in range(4):
+            nc.sync.dma_start(
+                bytes_in[r:P:4, :].bitcast(I32),
+                rows[r].unsqueeze(1).to_broadcast([4, 8, T // 4]),
+            )
+        w1_raw = load_weight("w1_raw", w1)
+        words_in = keep.tile([P, T], I32, name="words_in", align_bytes=64)
+        nc.sync.dma_start(words_in[:], x_words[0].rearrange("p c r -> p (c r)").bitcast(I32))
+
+        rates = keep.tile([P, 2, 8], F32, name="rates")
+        load_column(nc.scalar, rates[:, 0, 0:PACK], tau)
+        load_column(nc.scalar, rates[:, 1, 0:PACK], tau2)
+        gain = keep.tile([P, PACK], F32, name="gain")
+        load_column(nc.gpsimd, gain[:], gn)
+        slope = keep.tile([P, PACK], F32, name="slope")
+        load_column(nc.gpsimd, slope[:], sl)
+        thresh = keep.tile([P, PACK], F32, name="thresh")
+        load_column(nc.gpsimd, thresh[:], th)
+
+        n1_t = load_list("n1_t", n1)
+        n2_t = load_list("n2_t", n2)
+        two_t = load_list("two_t", two)
+        n3_t = load_list("n3_t", n3)
+        n4_t = load_list("n4_t", n4)
+
+        neg_rates = keep.tile([P, 2, PACK], F32, name="neg_rates")
+        nc.scalar.mul(neg_rates[:], rates[:, :, 0:PACK], -1.0)
+
+        bytes_offs = keep.tile([P, S], U8, name="bytes_offs", align_bytes=64)
+        nc.vector.tensor_copy(bytes_offs[:], bytes_in[:].indirect(offs_t[:]))
+        x_plane = keep.tile([P, S], U8, name="x_plane", align_bytes=64)
+        nc.vector.tensor_copy(x_plane[:].bitcast(I32), bytes_offs[:].bitcast(I32))
+        for r in range(2, 4):
+            nc.sync.dma_start(x_plane[r:P:32, :].bitcast(I32), bytes_offs[16 + r:P:32, :].bitcast(I32))
+
+        w1_q = quantize("w1", round_weight("w1_bf", w1_raw)[:].rearrange("p t m j -> p (t m j)"))
+        words_offs = keep.tile([P, S], U32, name="words_offs", tag="picked_words", align_bytes=64)
+        halves = [slice(0, S // 2), slice(S // 2, S)]
+        for i, cols in enumerate(halves):
+            nc.vector.tensor_copy(
+                words_offs[:, cols], words_in[:].bitcast(U32).indirect(offs_t[:, 16 * i:16 * (i + 1)]))
+
+        spent = keep.tile([P, PACK, 2, S], F32, name="exps", tag="scalar_out")
+        y_half = keep.tile([P, PACK, S], F32, name="y_half")
+        for t in range(PACK):
+            y = keep.tile([P, WIDE], F32, name="y%d" % t, tag="window%d" % t)
+            tops = keep.tile([P, 2], F32, name="tops%d" % t)
+            for i, cols in enumerate(halves):
+                bank = psum.tile([P, S // 2], F32, name="y_bank%d_%d" % (t, i), tag="bank%d" % (2 * t + i))
+                mx(bank[:], w1_q, t, (words_offs[:, cols], x_plane[:, cols]), True, True)
+                nc.vector.tensor_scalar(
+                    y[:, cols], bank[:], 1.0, None, ALU.mult, ALU.max, accum_out=tops[:, i:i + 1])
+            bias = keep.tile([P, 2], F32, name="bias%d" % t)
+            for u, lst in ((1, n2_t), (0, n1_t)):
+                nc.gpsimd.tensor_scalar(
+                    bias[:, u:u + 1], tops[:, 0:1], tops[:, 1:2], neg_rates[:, u, t:t + 1], ALU.max, ALU.mult)
+                nc.scalar.activation(
+                    spent[:, t, u, :], y[:].indirect(lst[:]), ACT.Exp,
+                    bias=bias[:, u:u + 1], scale=rates[:, u, t:t + 1],
+                )
+            nc.vector.tensor_scalar(y_half[:, t, :], y[:, 0:S], gain[:, t:t + 1], 0.5, ALU.mult, ALU.mult)
+
+        words_two = keep.tile([P, S], U32, name="words_two", tag="picked_words", align_bytes=64)
+        nc.vector.tensor_copy(words_two[:], words_in[:].bitcast(U32).indirect(two_t[:]))
+        bytes_two = keep.tile([P, S], U8, name="bytes_two", align_bytes=64)
+        nc.vector.tensor_copy(bytes_two[:], bytes_in[:].indirect(two_t[:]))
+        w3_bf = round_weight("w3_bf", load_weight("w3_raw", w3))
+        w2_bf = round_weight("w2_bf", load_weight("w2_raw", w2))
+        tab_rows = tab.rearrange("(p t) c -> t p c", t=PACK)
+        tab_t = []
+        for t in range(PACK):
+            window = keep.tile([P, WIDE], F32, name="tab%d" % t, tag="window%d" % t if t < 3 else "weight_raw")
+            nc.sync.dma_start(window[:, 0:J], tab_rows[t])
+            tab_t.append(window)
+        w3_q = quantize("w3", w3_bf[:].rearrange("p t m j -> p (t m j)"))
+        w2_q = quantize("w2", w2_bf[:].rearrange("p t m j -> p (t m j)"))
+        h_banks = [psum.tile([P, S], F32, name="h_bank%d" % t, tag="bank%d" % t) for t in range(PACK)]
+        for t in range(PACK):
+            mx(h_banks[t][:], w3_q, t, (words_two[:], bytes_two[:]), True, False)
+        sig_bias = keep.tile([P, PACK], F32, name="sig_bias")
+        slope_thresh = keep.tile([P, PACK], F32, name="slope_thresh")
+        nc.gpsimd.tensor_tensor(slope_thresh[:], slope[:], thresh[:], ALU.mult)
+        nc.gpsimd.tensor_scalar(sig_bias[:], slope_thresh[:], -1.0, 0.0, ALU.mult, ALU.add)
+
+        logs = keep.tile([P, PACK, 2, S], F32, name="logs", tag="window3")
+        part = keep.tile([P, PACK, S], F32, name="part")
+        z = keep.tile([P, PACK, S], F32, name="z")
+        for t in range(PACK):
+            for u in (1, 0):
+                nc.scalar.activation(logs[:, t, u, :], spent[:, t, u, :], ACT.Ln, bias=quarter[:])
+            nc.vector.scalar_tensor_tensor(
+                part[:, t, :], logs[:, t, 1, :], gain[:, t:t + 1], y_half[:, t, :], ALU.mult, ALU.subtract)
+            nc.vector.scalar_tensor_tensor(
+                z[:, t, :], logs[:, t, 0, :], gain[:, t:t + 1], part[:, t, :], ALU.mult, ALU.subtract)
+        z_bf = keep.tile([P, S, PACK], BF16, name="z_bf", align_bytes=64)
+        z_codes = keep.tile([P, S], U32, name="z_codes", align_bytes=64)
+        z_scales = keep.tile([P, S], U8, name="z_scales", align_bytes=64)
+        for cols in halves:
+            nc.vector.tensor_copy(
+                out=z_bf[:, cols, :].rearrange("p (c i) t -> p c t i", i=4),
+                in_=z[:, :, cols].rearrange("p t (c i) -> p c t i", i=4),
+            )
+        for cols in halves:
+            nc.vector.quantize_mx(
+                out=z_codes[:, cols].bitcast(FP8X4), scales=z_scales[:, cols],
+                in_=z_bf[:, cols, :].rearrange("p c t -> p (c t)"))
+        for t in range(PACK):
+            for i, cols in enumerate(halves):
+                mx(h_banks[t][:, cols], w2_q, t, (z_codes[:, cols], z_scales[:, cols]), False, i == 1)
+
+        gate = keep.tile([P, PACK, S], F32, name="gate", tag="scalar_out")
+        out_rows = out.rearrange("(p t) c -> t p c", t=PACK)
+
+        def leave_psum(t):
+            nc.scalar.activation(
+                gate[:, t, :], tab_t[t][:].indirect(n3_t[:]), ACT.Sigmoid,
+                bias=sig_bias[:, t:t + 1], scale=slope[:, t:t + 1])
+            gated = keep.tile([P, S], F32, name="gated%d" % t)
+            nc.vector.tensor_tensor(gated[:], h_banks[t][:], gate[:, t, :], ALU.mult)
+            minus_half = keep.tile([P, H_WINDOW], F32, name="minus_half%d" % t)
+            nc.scalar.mul(minus_half[:, 0:S], h_banks[t][:], -0.5)
+            return gated, minus_half
+
+        def finish(t, gated, minus_half):
+            result = keep.tile([P, S], F32, name="result%d" % t)
+            nc.vector.tensor_tensor(result[:], minus_half[:].indirect(n4_t[:]), gated[:], ALU.add)
+            nc.sync.dma_start(out_rows[t], result[:])
+
+        waiting = leave_psum(0)
+        for t in range(1, PACK):
+            ahead = leave_psum(t)
+            finish(t - 1, *waiting)
+            waiting = ahead
+        finish(PACK - 1, *waiting)

@@ -19,6 +19,8 @@ P = 128
 PACK = 4
 WIDE = 2 * S
 H_WINDOW = S + 16
+W1_SPLIT = 88
+Z_SPLIT = 352
 
 
 def tile_picked_hmixeosekd_none_p_kernel(
@@ -72,64 +74,91 @@ def tile_picked_hmixeosekd_none_p_kernel(
         quarter = keep.tile([P, 1], F32, name="quarter")
         nc.vector.memset(quarter[:], 0.25)
 
+        tab_rows = tab.rearrange("(p t) c -> t p c", t=PACK)
+
+        def load_tab(t):
+            window = keep.tile([P, WIDE], F32, name="tab%d" % t)
+            nc.sync.dma_start(window[:, 0:J], tab_rows[t])
+            return window
+
+        slope = keep.tile([P, PACK], F32, name="slope")
+        load_column(nc.scalar, slope[:], sl)
+        thresh = keep.tile([P, PACK], F32, name="thresh")
+        load_column(nc.scalar, thresh[:], th)
+        n3_t = load_list("n3_t", n3)
+        tab_t = [load_tab(0)]
         offs_t = load_list("offs_t", offs)
-        rows = x_scales[0].bitcast(I32).rearrange("(q r) c -> r q c", r=4)
-        for r in range(4):
-            nc.sync.dma_start(
-                bytes_in[r:P:4, :].bitcast(I32),
-                rows[r].unsqueeze(1).to_broadcast([4, 8, T // 4]),
-            )
-        w1_raw = load_weight("w1_raw", w1)
+        nc.sync.dma_start(
+            bytes_in[:].bitcast(I32), x_scales[0].bitcast(I32).unsqueeze(1).to_broadcast([16, 8, T // 4]))
+        tab_t.append(load_tab(1))
         words_in = keep.tile([P, T], I32, name="words_in", align_bytes=64)
         nc.sync.dma_start(words_in[:], x_words[0].rearrange("p c r -> p (c r)").bitcast(I32))
-
-        rates = keep.tile([P, 2, 8], F32, name="rates")
-        load_column(nc.scalar, rates[:, 0, 0:PACK], tau)
-        load_column(nc.scalar, rates[:, 1, 0:PACK], tau2)
-        gain = keep.tile([P, PACK], F32, name="gain")
-        load_column(nc.gpsimd, gain[:], gn)
-        slope = keep.tile([P, PACK], F32, name="slope")
-        load_column(nc.gpsimd, slope[:], sl)
-        thresh = keep.tile([P, PACK], F32, name="thresh")
-        load_column(nc.gpsimd, thresh[:], th)
-
-        n1_t = load_list("n1_t", n1)
+        tab_t.append(load_tab(2))
+        w1_raw = load_weight("w1_raw", w1)
+        tab_t.append(load_tab(3))
         n2_t = load_list("n2_t", n2)
+        n1_t = load_list("n1_t", n1)
         two_t = load_list("two_t", two)
-        n3_t = load_list("n3_t", n3)
         n4_t = load_list("n4_t", n4)
 
-        neg_rates = keep.tile([P, 2, PACK], F32, name="neg_rates")
-        nc.scalar.mul(neg_rates[:], rates[:, :, 0:PACK], -1.0)
+        rates = keep.tile([P, 2, 8], F32, name="rates")
+        load_column(nc.gpsimd, rates[:, 0, 0:PACK], tau)
+        load_column(nc.gpsimd, rates[:, 1, 0:PACK], tau2)
+        gain = keep.tile([P, PACK], F32, name="gain")
+        load_column(nc.gpsimd, gain[:], gn)
 
-        bytes_offs = keep.tile([P, S], U8, name="bytes_offs", align_bytes=64)
-        nc.vector.tensor_copy(bytes_offs[:], bytes_in[:].indirect(offs_t[:]))
-        x_plane = keep.tile([P, S], U8, name="x_plane", align_bytes=64)
-        nc.vector.tensor_copy(x_plane[:].bitcast(I32), bytes_offs[:].bitcast(I32))
-        for r in range(2, 4):
-            nc.sync.dma_start(x_plane[r:P:32, :].bitcast(I32), bytes_offs[16 + r:P:32, :].bitcast(I32))
+        sig_bias = keep.tile([P, PACK], F32, name="sig_bias")
+        nc.vector.scalar_tensor_tensor(sig_bias[:], slope[:], -1.0, thresh[:], ALU.mult, ALU.mult)
+        gate = keep.tile([P, PACK, S], F32, name="gate")
 
-        w1_q = quantize("w1", round_weight("w1_bf", w1_raw)[:].rearrange("p t m j -> p (t m j)"))
+        def make_gate(t):
+            nc.scalar.activation(
+                gate[:, t, :], tab_t[t][:].indirect(n3_t[:]), ACT.Sigmoid,
+                bias=sig_bias[:, t:t + 1], scale=slope[:, t:t + 1])
+
+        for t in range(PACK - 1):
+            make_gate(t)
+
+        def pick_scales(name, tag, lst, queue):
+            picked = keep.tile([P, S], U8, name=name + "_picked", tag=tag, align_bytes=64)
+            nc.vector.tensor_copy(picked[:], bytes_in[:].indirect(lst[:]))
+            plane = keep.tile([P, S], U8, name=name + "_plane", align_bytes=64)
+            nc.vector.tensor_copy(plane[:].bitcast(I32), picked[:].bitcast(I32))
+            for r in range(1, 4):
+                queue.dma_start(plane[r:P:32, :].bitcast(I32), picked[8 * r:P:32, :].bitcast(I32))
+            return plane
+
+        x_plane = pick_scales("offs", "offs_picked", offs_t, nc.scalar)
         words_offs = keep.tile([P, S], U32, name="words_offs", tag="picked_words", align_bytes=64)
-        halves = [slice(0, S // 2), slice(S // 2, S)]
-        for i, cols in enumerate(halves):
-            nc.vector.tensor_copy(
-                words_offs[:, cols], words_in[:].bitcast(U32).indirect(offs_t[:, 16 * i:16 * (i + 1)]))
+        nc.vector.tensor_copy(words_offs[:], words_in[:].bitcast(U32).indirect(offs_t[:]))
 
-        spent = keep.tile([P, PACK, 2, S], F32, name="exps", tag="scalar_out")
+        w1_bf = keep.tile([P, PACK, P, PACK], BF16, name="w1_bf", align_bytes=64)
+        w1_dst = w1_bf[:].rearrange("p t m j -> p m j t")
+        w1_src = w1_raw[:].rearrange("p j (m t) -> p m j t", t=PACK)
+        nc.vector.tensor_copy(out=w1_dst[:, 0:W1_SPLIT], in_=w1_src[:, 0:W1_SPLIT])
+        nc.scalar.copy(out=w1_dst[:, W1_SPLIT:P], in_=w1_src[:, W1_SPLIT:P])
+        w1_q = (keep.tile([P, H], U32, name="w1_codes", align_bytes=64),
+                keep.tile([P, H], U8, name="w1_scales", align_bytes=64))
+        for t0, t1 in ((0, 1), (1, 2), (2, 4)):
+            nc.vector.quantize_mx(
+                out=w1_q[0][:, t0 * P:t1 * P].bitcast(FP8X4), scales=w1_q[1][:, t0 * P:t1 * P],
+                in_=w1_bf[:, t0:t1].rearrange("p t m j -> p (t m j)"))
+
+        make_gate(PACK - 1)
+        warm = keep.tile([P, 1], F32, name="warm")
+        nc.scalar.activation(warm[:], gate[:, PACK - 1, 0:1], ACT.Exp)
+
+        spent = keep.tile([P, PACK, 2, S], F32, name="exps")
         y_half = keep.tile([P, PACK, S], F32, name="y_half")
         for t in range(PACK):
+            bank = psum.tile([P, S], F32, name="y_bank%d" % t)
+            mx(bank[:], w1_q, t, (words_offs[:], x_plane[:]), True, True)
             y = keep.tile([P, WIDE], F32, name="y%d" % t, tag="window%d" % t)
-            tops = keep.tile([P, 2], F32, name="tops%d" % t)
-            for i, cols in enumerate(halves):
-                bank = psum.tile([P, S // 2], F32, name="y_bank%d_%d" % (t, i), tag="bank%d" % (2 * t + i))
-                mx(bank[:], w1_q, t, (words_offs[:, cols], x_plane[:, cols]), True, True)
-                nc.vector.tensor_scalar(
-                    y[:, cols], bank[:], 1.0, None, ALU.mult, ALU.max, accum_out=tops[:, i:i + 1])
+            top = keep.tile([P, 1], F32, name="top%d" % t)
+            nc.vector.tensor_scalar(y[:, 0:S], bank[:], 1.0, None, ALU.mult, ALU.max, accum_out=top[:])
             bias = keep.tile([P, 2], F32, name="bias%d" % t)
+            nc.vector.tensor_scalar(bias[:], rates[:, :, t], top[:], -1.0, ALU.mult, ALU.mult)
             for u, lst in ((1, n2_t), (0, n1_t)):
-                nc.gpsimd.tensor_scalar(
-                    bias[:, u:u + 1], tops[:, 0:1], tops[:, 1:2], neg_rates[:, u, t:t + 1], ALU.max, ALU.mult)
                 nc.scalar.activation(
                     spent[:, t, u, :], y[:].indirect(lst[:]), ACT.Exp,
                     bias=bias[:, u:u + 1], scale=rates[:, u, t:t + 1],
@@ -138,25 +167,14 @@ def tile_picked_hmixeosekd_none_p_kernel(
 
         words_two = keep.tile([P, S], U32, name="words_two", tag="picked_words", align_bytes=64)
         nc.vector.tensor_copy(words_two[:], words_in[:].bitcast(U32).indirect(two_t[:]))
-        bytes_two = keep.tile([P, S], U8, name="bytes_two", align_bytes=64)
-        nc.vector.tensor_copy(bytes_two[:], bytes_in[:].indirect(two_t[:]))
+        bytes_two = pick_scales("two", "offs_plane", two_t, nc.sync)
         w3_bf = round_weight("w3_bf", load_weight("w3_raw", w3))
         w2_bf = round_weight("w2_bf", load_weight("w2_raw", w2))
-        tab_rows = tab.rearrange("(p t) c -> t p c", t=PACK)
-        tab_t = []
-        for t in range(PACK):
-            window = keep.tile([P, WIDE], F32, name="tab%d" % t, tag="window%d" % t if t < 3 else "weight_raw")
-            nc.sync.dma_start(window[:, 0:J], tab_rows[t])
-            tab_t.append(window)
         w3_q = quantize("w3", w3_bf[:].rearrange("p t m j -> p (t m j)"))
         w2_q = quantize("w2", w2_bf[:].rearrange("p t m j -> p (t m j)"))
-        h_banks = [psum.tile([P, S], F32, name="h_bank%d" % t, tag="bank%d" % t) for t in range(PACK)]
+        h_banks = [psum.tile([P, S], F32, name="h_bank%d" % t) for t in range(PACK)]
         for t in range(PACK):
             mx(h_banks[t][:], w3_q, t, (words_two[:], bytes_two[:]), True, False)
-        sig_bias = keep.tile([P, PACK], F32, name="sig_bias")
-        slope_thresh = keep.tile([P, PACK], F32, name="slope_thresh")
-        nc.gpsimd.tensor_tensor(slope_thresh[:], slope[:], thresh[:], ALU.mult)
-        nc.gpsimd.tensor_scalar(sig_bias[:], slope_thresh[:], -1.0, 0.0, ALU.mult, ALU.add)
 
         logs = keep.tile([P, PACK, 2, S], F32, name="logs", tag="window3")
         part = keep.tile([P, PACK, S], F32, name="part")
@@ -171,8 +189,13 @@ def tile_picked_hmixeosekd_none_p_kernel(
         z_bf = keep.tile([P, S, PACK], BF16, name="z_bf", align_bytes=64)
         z_codes = keep.tile([P, S], U32, name="z_codes", align_bytes=64)
         z_scales = keep.tile([P, S], U8, name="z_scales", align_bytes=64)
-        for cols in halves:
-            nc.vector.tensor_copy(
+        halves = [slice(0, S // 2), slice(S // 2, S)]
+        for copy, cols in (
+            (nc.vector.tensor_copy, slice(0, S // 2)),
+            (nc.scalar.copy, slice(Z_SPLIT, S)),
+            (nc.vector.tensor_copy, slice(S // 2, Z_SPLIT)),
+        ):
+            copy(
                 out=z_bf[:, cols, :].rearrange("p (c i) t -> p c t i", i=4),
                 in_=z[:, :, cols].rearrange("p t (c i) -> p c t i", i=4),
             )
@@ -184,13 +207,9 @@ def tile_picked_hmixeosekd_none_p_kernel(
             for i, cols in enumerate(halves):
                 mx(h_banks[t][:, cols], w2_q, t, (z_codes[:, cols], z_scales[:, cols]), False, i == 1)
 
-        gate = keep.tile([P, PACK, S], F32, name="gate", tag="scalar_out")
         out_rows = out.rearrange("(p t) c -> t p c", t=PACK)
 
         def leave_psum(t):
-            nc.scalar.activation(
-                gate[:, t, :], tab_t[t][:].indirect(n3_t[:]), ACT.Sigmoid,
-                bias=sig_bias[:, t:t + 1], scale=slope[:, t:t + 1])
             gated = keep.tile([P, S], F32, name="gated%d" % t)
             nc.vector.tensor_tensor(gated[:], h_banks[t][:], gate[:, t, :], ALU.mult)
             minus_half = keep.tile([P, H_WINDOW], F32, name="minus_half%d" % t)
@@ -202,9 +221,21 @@ def tile_picked_hmixeosekd_none_p_kernel(
             nc.vector.tensor_tensor(result[:], minus_half[:].indirect(n4_t[:]), gated[:], ALU.add)
             nc.sync.dma_start(out_rows[t], result[:])
 
-        waiting = leave_psum(0)
-        for t in range(1, PACK):
-            ahead = leave_psum(t)
-            finish(t - 1, *waiting)
-            waiting = ahead
-        finish(PACK - 1, *waiting)
+        def fetch(t, minus_half):
+            fetched = keep.tile([P, S], F32, name="fetched%d" % t)
+            nc.scalar.activation(fetched[:], minus_half[:].indirect(n4_t[:]), ACT.Copy)
+            return fetched
+
+        def add_fetched(t, gated, fetched):
+            result = keep.tile([P, S], F32, name="result%d" % t)
+            nc.vector.tensor_tensor(result[:], fetched[:], gated[:], ALU.add)
+            nc.sync.dma_start(out_rows[t], result[:])
+
+        left = [leave_psum(0), leave_psum(1)]
+        finish(0, *left[0])
+        fetched = fetch(1, left[1][1])
+        left.append(leave_psum(2))
+        left.append(leave_psum(3))
+        add_fetched(1, left[1][0], fetched)
+        finish(2, *left[2])
+        add_fetched(3, left[3][0], fetch(3, left[3][1]))

@@ -39,8 +39,8 @@ def tile_picked_hmixeosekd_none_p_kernel(
         def load_column(queue, dst, src):
             queue.dma_start(dst, src.rearrange("(p t) o -> p (t o)", t=PACK))
 
-        def load_weight(name, src):
-            raw = keep.tile([P, PACK, 512], F32, name=name, tag="weight_raw")
+        def load_weight(name, tag, src):
+            raw = keep.tile([P, PACK, 512], F32, name=name, tag=tag)
             nc.sync.dma_start(raw[:], src.rearrange("(p j) c -> p j c", j=PACK))
             return raw
 
@@ -88,17 +88,17 @@ def tile_picked_hmixeosekd_none_p_kernel(
         n3_t = load_list("n3_t", n3)
         tab_t = [load_tab(0)]
         offs_t = load_list("offs_t", offs)
+        two_t = load_list("two_t", two)
         nc.sync.dma_start(
             bytes_in[:].bitcast(I32), x_scales[0].bitcast(I32).unsqueeze(1).to_broadcast([16, 8, T // 4]))
         tab_t.append(load_tab(1))
         words_in = keep.tile([P, T], I32, name="words_in", align_bytes=64)
         nc.sync.dma_start(words_in[:], x_words[0].rearrange("p c r -> p (c r)").bitcast(I32))
         tab_t.append(load_tab(2))
-        w1_raw = load_weight("w1_raw", w1)
+        w1_raw = load_weight("w1_raw", "w1_raw", w1)
         tab_t.append(load_tab(3))
         n2_t = load_list("n2_t", n2)
         n1_t = load_list("n1_t", n1)
-        two_t = load_list("two_t", two)
         n4_t = load_list("n4_t", n4)
 
         rates = keep.tile([P, 2, 8], F32, name="rates")
@@ -119,8 +119,8 @@ def tile_picked_hmixeosekd_none_p_kernel(
         for t in range(PACK - 1):
             make_gate(t)
 
-        def pick_scales(name, tag, lst, queue):
-            picked = keep.tile([P, S], U8, name=name + "_picked", tag=tag, align_bytes=64)
+        def pick_scales(name, lst, queue):
+            picked = keep.tile([P, S], U8, name=name + "_picked", align_bytes=64)
             nc.vector.tensor_copy(picked[:], bytes_in[:].indirect(lst[:]))
             plane = keep.tile([P, S], U8, name=name + "_plane", align_bytes=64)
             nc.vector.tensor_copy(plane[:].bitcast(I32), picked[:].bitcast(I32))
@@ -128,9 +128,12 @@ def tile_picked_hmixeosekd_none_p_kernel(
                 queue.dma_start(plane[r:P:32, :].bitcast(I32), picked[8 * r:P:32, :].bitcast(I32))
             return plane
 
-        x_plane = pick_scales("offs", "offs_picked", offs_t, nc.scalar)
-        words_offs = keep.tile([P, S], U32, name="words_offs", tag="picked_words", align_bytes=64)
+        x_plane = pick_scales("offs", offs_t, nc.scalar)
+        bytes_two = pick_scales("two", two_t, nc.sync)
+        words_offs = keep.tile([P, S], U32, name="words_offs", align_bytes=64)
         nc.vector.tensor_copy(words_offs[:], words_in[:].bitcast(U32).indirect(offs_t[:]))
+        words_two = keep.tile([P, S], U32, name="words_two", align_bytes=64)
+        nc.vector.tensor_copy(words_two[:], words_in[:].bitcast(U32).indirect(two_t[:]))
 
         w1_bf = keep.tile([P, PACK, P, PACK], BF16, name="w1_bf", align_bytes=64)
         w1_dst = w1_bf[:].rearrange("p t m j -> p m j t")
@@ -151,7 +154,7 @@ def tile_picked_hmixeosekd_none_p_kernel(
         spent = keep.tile([P, PACK, 2, S], F32, name="exps")
         y_half = keep.tile([P, PACK, S], F32, name="y_half")
         for t in range(PACK):
-            bank = psum.tile([P, S], F32, name="y_bank%d" % t)
+            bank = psum.tile([P, S], F32, name="y_bank")
             mx(bank[:], w1_q, t, (words_offs[:], x_plane[:]), True, True)
             y = keep.tile([P, WIDE], F32, name="y%d" % t, tag="window%d" % t)
             top = keep.tile([P, 1], F32, name="top%d" % t)
@@ -165,11 +168,8 @@ def tile_picked_hmixeosekd_none_p_kernel(
                 )
             nc.vector.tensor_scalar(y_half[:, t, :], y[:, 0:S], gain[:, t:t + 1], 0.5, ALU.mult, ALU.mult)
 
-        words_two = keep.tile([P, S], U32, name="words_two", tag="picked_words", align_bytes=64)
-        nc.vector.tensor_copy(words_two[:], words_in[:].bitcast(U32).indirect(two_t[:]))
-        bytes_two = pick_scales("two", "offs_plane", two_t, nc.sync)
-        w3_bf = round_weight("w3_bf", load_weight("w3_raw", w3))
-        w2_bf = round_weight("w2_bf", load_weight("w2_raw", w2))
+        w3_bf = round_weight("w3_bf", load_weight("w3_raw", "w1_raw", w3))
+        w2_bf = round_weight("w2_bf", load_weight("w2_raw", "tab3", w2))
         w3_q = quantize("w3", w3_bf[:].rearrange("p t m j -> p (t m j)"))
         w2_q = quantize("w2", w2_bf[:].rearrange("p t m j -> p (t m j)"))
         h_banks = [psum.tile([P, S], F32, name="h_bank%d" % t) for t in range(PACK)]
@@ -179,13 +179,22 @@ def tile_picked_hmixeosekd_none_p_kernel(
         logs = keep.tile([P, PACK, 2, S], F32, name="logs", tag="window3")
         part = keep.tile([P, PACK, S], F32, name="part")
         z = keep.tile([P, PACK, S], F32, name="z")
-        for t in range(PACK):
-            for u in (1, 0):
-                nc.scalar.activation(logs[:, t, u, :], spent[:, t, u, :], ACT.Ln, bias=quarter[:])
+
+        def subtrahend(t):
+            nc.scalar.activation(logs[:, t, 1, :], spent[:, t, 1, :], ACT.Ln, bias=quarter[:])
             nc.vector.scalar_tensor_tensor(
                 part[:, t, :], logs[:, t, 1, :], gain[:, t:t + 1], y_half[:, t, :], ALU.mult, ALU.subtract)
+
+        def minuend(t):
+            nc.scalar.activation(logs[:, t, 0, :], spent[:, t, 0, :], ACT.Ln, bias=quarter[:])
             nc.vector.scalar_tensor_tensor(
                 z[:, t, :], logs[:, t, 0, :], gain[:, t:t + 1], part[:, t, :], ALU.mult, ALU.subtract)
+
+        subtrahend(0)
+        for t in range(1, PACK):
+            subtrahend(t)
+            minuend(t - 1)
+        minuend(PACK - 1)
         z_bf = keep.tile([P, S, PACK], BF16, name="z_bf", align_bytes=64)
         z_codes = keep.tile([P, S], U32, name="z_codes", align_bytes=64)
         z_scales = keep.tile([P, S], U8, name="z_scales", align_bytes=64)
@@ -204,8 +213,7 @@ def tile_picked_hmixeosekd_none_p_kernel(
                 out=z_codes[:, cols].bitcast(FP8X4), scales=z_scales[:, cols],
                 in_=z_bf[:, cols, :].rearrange("p c t -> p (c t)"))
         for t in range(PACK):
-            for i, cols in enumerate(halves):
-                mx(h_banks[t][:, cols], w2_q, t, (z_codes[:, cols], z_scales[:, cols]), False, i == 1)
+            mx(h_banks[t][:], w2_q, t, (z_codes[:], z_scales[:]), False, True)
 
         out_rows = out.rearrange("(p t) c -> t p c", t=PACK)
 
@@ -223,12 +231,15 @@ def tile_picked_hmixeosekd_none_p_kernel(
 
         def fetch(t, minus_half):
             fetched = keep.tile([P, S], F32, name="fetched%d" % t)
-            nc.scalar.activation(fetched[:], minus_half[:].indirect(n4_t[:]), ACT.Copy)
+            for i, cols in enumerate(halves):
+                nc.scalar.activation(
+                    fetched[:, cols], minus_half[:].indirect(n4_t[:, 16 * i:16 * (i + 1)]), ACT.Copy)
             return fetched
 
         def add_fetched(t, gated, fetched):
             result = keep.tile([P, S], F32, name="result%d" % t)
-            nc.vector.tensor_tensor(result[:], fetched[:], gated[:], ALU.add)
+            for cols in halves:
+                nc.vector.tensor_tensor(result[:, cols], fetched[:, cols], gated[:, cols], ALU.add)
             nc.sync.dma_start(out_rows[t], result[:])
 
         left = [leave_psum(0), leave_psum(1)]

@@ -119,17 +119,17 @@ def tile_picked_hmixeosekd_none_p_kernel(
         for t in range(PACK - 1):
             make_gate(t)
 
-        def pick_scales(name, lst, queue):
+        def pick_scales(name, lst):
             picked = keep.tile([P, S], U8, name=name + "_picked", align_bytes=64)
             nc.vector.tensor_copy(picked[:], bytes_in[:].indirect(lst[:]))
             plane = keep.tile([P, S], U8, name=name + "_plane", align_bytes=64)
             nc.vector.tensor_copy(plane[:].bitcast(I32), picked[:].bitcast(I32))
             for r in range(1, 4):
-                queue.dma_start(plane[r:P:32, :].bitcast(I32), picked[8 * r:P:32, :].bitcast(I32))
+                nc.sync.dma_start(plane[r:P:32, :].bitcast(I32), picked[8 * r:P:32, :].bitcast(I32))
             return plane
 
-        x_plane = pick_scales("offs", offs_t, nc.scalar)
-        bytes_two = pick_scales("two", two_t, nc.sync)
+        x_plane = pick_scales("offs", offs_t)
+        bytes_two = pick_scales("two", two_t)
         words_offs = keep.tile([P, S], U32, name="words_offs", align_bytes=64)
         nc.vector.tensor_copy(words_offs[:], words_in[:].bitcast(U32).indirect(offs_t[:]))
         words_two = keep.tile([P, S], U32, name="words_two", align_bytes=64)
@@ -154,10 +154,10 @@ def tile_picked_hmixeosekd_none_p_kernel(
         spent = keep.tile([P, PACK, 2, S], F32, name="exps")
         y_half = keep.tile([P, PACK, S], F32, name="y_half")
         for t in range(PACK):
-            bank = psum.tile([P, S], F32, name="y_bank")
+            bank = psum.tile([P, S], F32, name="y_bank%d" % t)
             mx(bank[:], w1_q, t, (words_offs[:], x_plane[:]), True, True)
             y = keep.tile([P, WIDE], F32, name="y%d" % t, tag="window%d" % t)
-            top = keep.tile([P, 1], F32, name="top%d" % t)
+            top = keep.tile([P, 1], F32, name="top%d" % t, tag="window%d" % (t + 1))
             nc.vector.tensor_scalar(y[:, 0:S], bank[:], 1.0, None, ALU.mult, ALU.max, accum_out=top[:])
             bias = keep.tile([P, 2], F32, name="bias%d" % t)
             nc.vector.tensor_scalar(bias[:], rates[:, :, t], top[:], -1.0, ALU.mult, ALU.mult)
@@ -229,24 +229,17 @@ def tile_picked_hmixeosekd_none_p_kernel(
             nc.vector.tensor_tensor(result[:], minus_half[:].indirect(n4_t[:]), gated[:], ALU.add)
             nc.sync.dma_start(out_rows[t], result[:])
 
-        def fetch(t, minus_half):
+        def finish_split(t, gated, minus_half):
             fetched = keep.tile([P, S], F32, name="fetched%d" % t)
+            result = keep.tile([P, S], F32, name="result%d" % t)
             for i, cols in enumerate(halves):
                 nc.scalar.activation(
                     fetched[:, cols], minus_half[:].indirect(n4_t[:, 16 * i:16 * (i + 1)]), ACT.Copy)
-            return fetched
-
-        def add_fetched(t, gated, fetched):
-            result = keep.tile([P, S], F32, name="result%d" % t)
-            for cols in halves:
                 nc.vector.tensor_tensor(result[:, cols], fetched[:, cols], gated[:, cols], ALU.add)
-            nc.sync.dma_start(out_rows[t], result[:])
+                nc.sync.dma_start(out_rows[t][:, cols], result[:, cols])
 
-        left = [leave_psum(0), leave_psum(1)]
+        left = [leave_psum(t) for t in range(PACK)]
         finish(0, *left[0])
-        fetched = fetch(1, left[1][1])
-        left.append(leave_psum(2))
-        left.append(leave_psum(3))
-        add_fetched(1, left[1][0], fetched)
         finish(2, *left[2])
-        add_fetched(3, left[3][0], fetch(3, left[3][1]))
+        finish_split(1, *left[1])
+        finish_split(3, *left[3])

@@ -148,8 +148,6 @@ def tile_picked_hmixeosekd_none_p_kernel(
                 in_=w1_bf[:, t0:t1].rearrange("p t m j -> p (t m j)"))
 
         make_gate(PACK - 1)
-        warm = keep.tile([P, 1], F32, name="warm")
-        nc.scalar.activation(warm[:], gate[:, PACK - 1, 0:1], ACT.Exp)
 
         spent = keep.tile([P, PACK, 2, S], F32, name="exps")
         y_half = keep.tile([P, PACK, S], F32, name="y_half")

from contextlib import ExitStack

import concourse.mybir as mybir

K, T, S, N, H, J = 512, 2048, 512, 512, 512, 512
FLOPS = 3 * 2 * 512 * 512 * 512

F32 = mybir.dt.float32
BF16 = mybir.dt.bfloat16
I32 = mybir.dt.int32
U32 = mybir.dt.uint32
U16 = mybir.dt.uint16
U8 = mybir.dt.uint8
FP8X4 = mybir.dt.float8_e4m3fn_x4
ALU = mybir.AluOpType
ACT = mybir.ActivationFunctionType

P = 128
PACK = 4
WIDE = 2 * S
H_WINDOW = S + 16
W1_SPLIT = 88
Z_SPLIT = 352


def tile_picked_hmixeosekd_none_p_kernel(
    tc, x_words, x_scales, w1, tau, tau2, gn, w2, w3, tab, sl, th, offs, n1, n2, two, n3, n4, out
):
    nc = tc.nc
    with ExitStack() as ctx:
        keep = ctx.enter_context(tc.tile_pool(name="keep", bufs=1))
        psum = ctx.enter_context(tc.psum_pool(name="psum", bufs=1))

        def load_list(name, src):
            dst = keep.tile([P, S // 16], U16, name=name)
            nc.sync.dma_start(dst[:], src)
            return dst

        def load_column(queue, dst, src):
            queue.dma_start(dst, src.rearrange("(p t) o -> p (t o)", t=PACK))

        def load_weight(name, tag, src):
            raw = keep.tile([P, PACK, 512], F32, name=name, tag=tag)
            nc.sync.dma_start(raw[:], src.rearrange("(p j) c -> p j c", j=PACK))
            return raw

        def round_weight(name, raw):
            grouped = keep.tile([P, PACK, P, PACK], BF16, name=name, align_bytes=64)
            nc.vector.tensor_copy(
                out=grouped[:].rearrange("p t m j -> p m j t"),
                in_=raw[:].rearrange("p j (m t) -> p m j t", t=PACK),
            )
            return grouped

        def quantize(name, grouped_ap):
            codes = keep.tile([P, 512], U32, name=name + "_codes", align_bytes=64)
            scales = keep.tile([P, 512], U8, name=name + "_scales", align_bytes=64)
            nc.vector.quantize_mx(out=codes[:].bitcast(FP8X4), scales=scales[:], in_=grouped_ap)
            return codes, scales

        def mx(bank, weight, t, moving, start, stop):
            cols = slice(t * P, (t + 1) * P)
            nc.tensor.matmul_mx(
                out=bank,
                lhsT=weight[0][:, cols].bitcast(FP8X4),
                lhsT_scale=weight[1][:, cols],
                rhs=moving[0].bitcast(FP8X4),
                rhs_scale=moving[1],
                start=start,
                stop=stop,
            )

        bytes_in = keep.tile([P, T], U8, name="bytes_in", align_bytes=64)
        quarter = keep.tile([P, 1], F32, name="quarter")
        nc.vector.memset(quarter[:], 0.25)

        tab_rows = tab.rearrange("(p t) c -> t p c", t=PACK)

        def load_tab(t):
            window = keep.tile([P, WIDE], F32, name="tab%d" % t)
            nc.sync.dma_start(window[:, 0:J], tab_rows[t])
            return window

        slope = keep.tile([P, PACK], F32, name="slope")
        load_column(nc.scalar, slope[:], sl)
        thresh = keep.tile([P, PACK], F32, name="thresh")
        load_column(nc.scalar, thresh[:], th)
        n3_t = load_list("n3_t", n3)
        tab_t = [load_tab(0)]
        offs_t = load_list("offs_t", offs)
        two_t = load_list("two_t", two)
        nc.sync.dma_start(
            bytes_in[:].bitcast(I32), x_scales[0].bitcast(I32).unsqueeze(1).to_broadcast([16, 8, T // 4]))
        tab_t.append(load_tab(1))
        words_in = keep.tile([P, T], I32, name="words_in", align_bytes=64)
        nc.sync.dma_start(words_in[:], x_words[0].rearrange("p c r -> p (c r)").bitcast(I32))
        tab_t.append(load_tab(2))
        w1_raw = load_weight("w1_raw", "w1_raw", w1)
        tab_t.append(load_tab(3))
        n2_t = load_list("n2_t", n2)
        n1_t = load_list("n1_t", n1)
        n4_t = load_list("n4_t", n4)

        rates = keep.tile([P, 2, 8], F32, name="rates")
        load_column(nc.gpsimd, rates[:, 0, 0:PACK], tau)
        load_column(nc.gpsimd, rates[:, 1, 0:PACK], tau2)
        gain = keep.tile([P, PACK], F32, name="gain")
        load_column(nc.gpsimd, gain[:], gn)

        sig_bias = keep.tile([P, PACK], F32, name="sig_bias")
        nc.vector.scalar_tensor_tensor(sig_bias[:], slope[:], -1.0, thresh[:], ALU.mult, ALU.mult)
        gate = keep.tile([P, PACK, S], F32, name="gate")

        def make_gate(t):
            nc.scalar.activation(
                gate[:, t, :], tab_t[t][:].indirect(n3_t[:]), ACT.Sigmoid,
                bias=sig_bias[:, t:t + 1], scale=slope[:, t:t + 1])

        for t in range(PACK - 1):
            make_gate(t)

        def pick_scales(name, lst):
            picked = keep.tile([P, S], U8, name=name + "_picked", align_bytes=64)
            nc.vector.tensor_copy(picked[:], bytes_in[:].indirect(lst[:]))
            plane = keep.tile([P, S], U8, name=name + "_plane", align_bytes=64)
            nc.vector.tensor_copy(plane[:].bitcast(I32), picked[:].bitcast(I32))
            for r in range(1, 4):
                nc.sync.dma_start(plane[r:P:32, :].bitcast(I32), picked[8 * r:P:32, :].bitcast(I32))
            return plane

        x_plane = pick_scales("offs", offs_t)
        bytes_two = pick_scales("two", two_t)
        words_offs = keep.tile([P, S], U32, name="words_offs", align_bytes=64)
        nc.vector.tensor_copy(words_offs[:], words_in[:].bitcast(U32).indirect(offs_t[:]))
        words_two = keep.tile([P, S], U32, name="words_two", align_bytes=64)
        nc.vector.tensor_copy(words_two[:], words_in[:].bitcast(U32).indirect(two_t[:]))

        w1_bf = keep.tile([P, PACK, P, PACK], BF16, name="w1_bf", align_bytes=64)
        w1_dst = w1_bf[:].rearrange("p t m j -> p m j t")
        w1_src = w1_raw[:].rearrange("p j (m t) -> p m j t", t=PACK)
        nc.vector.tensor_copy(out=w1_dst[:, 0:W1_SPLIT], in_=w1_src[:, 0:W1_SPLIT])
        nc.scalar.copy(out=w1_dst[:, W1_SPLIT:P], in_=w1_src[:, W1_SPLIT:P])
        w1_q = (keep.tile([P, H], U32, name="w1_codes", align_bytes=64),
                keep.tile([P, H], U8, name="w1_scales", align_bytes=64))
        for t0, t1 in ((0, 1), (1, 2), (2, 4)):
            nc.vector.quantize_mx(
                out=w1_q[0][:, t0 * P:t1 * P].bitcast(FP8X4), scales=w1_q[1][:, t0 * P:t1 * P],
                in_=w1_bf[:, t0:t1].rearrange("p t m j -> p (t m j)"))

        make_gate(PACK - 1)

        spent = keep.tile([P, PACK, 2, S], F32, name="exps")
        y_half = keep.tile([P, PACK, S], F32, name="y_half")
        for t in range(PACK):
            bank = psum.tile([P, S], F32, name="y_bank%d" % t)
            mx(bank[:], w1_q, t, (words_offs[:], x_plane[:]), True, True)
            y = keep.tile([P, WIDE], F32, name="y%d" % t, tag="window%d" % t)
            top = keep.tile([P, 1], F32, name="top%d" % t, tag="window%d" % (t + 1))
            nc.vector.tensor_scalar(y[:, 0:S], bank[:], 1.0, None, ALU.mult, ALU.max, accum_out=top[:])
            bias = keep.tile([P, 2], F32, name="bias%d" % t)
            nc.vector.tensor_scalar(bias[:], rates[:, :, t], top[:], -1.0, ALU.mult, ALU.mult)
            for u, lst in ((1, n2_t), (0, n1_t)):
                nc.scalar.activation(
                    spent[:, t, u, :], y[:].indirect(lst[:]), ACT.Exp,
                    bias=bias[:, u:u + 1], scale=rates[:, u, t:t + 1],
                )
            nc.vector.tensor_scalar(y_half[:, t, :], y[:, 0:S], gain[:, t:t + 1], 0.5, ALU.mult, ALU.mult)

        w3_bf = round_weight("w3_bf", load_weight("w3_raw", "w1_raw", w3))
        w2_bf = round_weight("w2_bf", load_weight("w2_raw", "tab3", w2))
        w3_q = quantize("w3", w3_bf[:].rearrange("p t m j -> p (t m j)"))
        w2_q = quantize("w2", w2_bf[:].rearrange("p t m j -> p (t m j)"))
        h_banks = [psum.tile([P, S], F32, name="h_bank%d" % t) for t in range(PACK)]
        for t in range(PACK):
            mx(h_banks[t][:], w3_q, t, (words_two[:], bytes_two[:]), True, False)

        logs = keep.tile([P, PACK, 2, S], F32, name="logs", tag="window3")
        part = keep.tile([P, PACK, S], F32, name="part")
        z = keep.tile([P, PACK, S], F32, name="z")

        def subtrahend(t):
            nc.scalar.activation(logs[:, t, 1, :], spent[:, t, 1, :], ACT.Ln, bias=quarter[:])
            nc.vector.scalar_tensor_tensor(
                part[:, t, :], logs[:, t, 1, :], gain[:, t:t + 1], y_half[:, t, :], ALU.mult, ALU.subtract)

        def minuend(t):
            nc.scalar.activation(logs[:, t, 0, :], spent[:, t, 0, :], ACT.Ln, bias=quarter[:])
            nc.vector.scalar_tensor_tensor(
                z[:, t, :], logs[:, t, 0, :], gain[:, t:t + 1], part[:, t, :], ALU.mult, ALU.subtract)

        subtrahend(0)
        for t in range(1, PACK):
            subtrahend(t)
            minuend(t - 1)
        minuend(PACK - 1)
        z_bf = keep.tile([P, S, PACK], BF16, name="z_bf", align_bytes=64)
        z_codes = keep.tile([P, S], U32, name="z_codes", align_bytes=64)
        z_scales = keep.tile([P, S], U8, name="z_scales", align_bytes=64)
        halves = [slice(0, S // 2), slice(S // 2, S)]
        for copy, cols in (
            (nc.vector.tensor_copy, slice(0, S // 2)),
            (nc.scalar.copy, slice(Z_SPLIT, S)),
            (nc.vector.tensor_copy, slice(S // 2, Z_SPLIT)),
        ):
            copy(
                out=z_bf[:, cols, :].rearrange("p (c i) t -> p c t i", i=4),
                in_=z[:, :, cols].rearrange("p t (c i) -> p c t i", i=4),
            )
        for cols in halves:
            nc.vector.quantize_mx(
                out=z_codes[:, cols].bitcast(FP8X4), scales=z_scales[:, cols],
                in_=z_bf[:, cols, :].rearrange("p c t -> p (c t)"))
        for t in range(PACK):
            mx(h_banks[t][:], w2_q, t, (z_codes[:], z_scales[:]), False, True)

        out_rows = out.rearrange("(p t) c -> t p c", t=PACK)

        def leave_psum(t):
            gated = keep.tile([P, S], F32, name="gated%d" % t)
            nc.vector.tensor_tensor(gated[:], h_banks[t][:], gate[:, t, :], ALU.mult)
            minus_half = keep.tile([P, H_WINDOW], F32, name="minus_half%d" % t)
            nc.scalar.mul(minus_half[:, 0:S], h_banks[t][:], -0.5)
            return gated, minus_half

        def finish(t, gated, minus_half):
            result = keep.tile([P, S], F32, name="result%d" % t)
            nc.vector.tensor_tensor(result[:], minus_half[:].indirect(n4_t[:]), gated[:], ALU.add)
            nc.sync.dma_start(out_rows[t], result[:])

        def finish_split(t, gated, minus_half):
            fetched = keep.tile([P, S], F32, name="fetched%d" % t)
            result = keep.tile([P, S], F32, name="result%d" % t)
            for i, cols in enumerate(halves):
                nc.scalar.activation(
                    fetched[:, cols], minus_half[:].indirect(n4_t[:, 16 * i:16 * (i + 1)]), ACT.Copy)
                nc.vector.tensor_tensor(result[:, cols], fetched[:, cols], gated[:, cols], ALU.add)
                nc.sync.dma_start(out_rows[t][:, cols], result[:, cols])

        left = [leave_psum(t) for t in range(PACK)]
        finish(0, *left[0])
        finish(2, *left[2])
        finish_split(1, *left[1])
        finish_split(3, *left[3])
